import numpy as np
import ml_dtypes


def mxq(x, axis, fmt="e4m3"):
    dtype, down = {"e4m3": (ml_dtypes.float8_e4m3fn, 7), "e5m2": (ml_dtypes.float8_e5m2, 14)}[fmt]
    v = np.moveaxis(np.asarray(x, np.float32).astype(ml_dtypes.bfloat16).astype(np.float64), axis, -1)
    blocks = v.reshape(v.shape[:-1] + (-1, 32))
    amax = np.abs(blocks).max(-1, keepdims=True)
    byte = np.maximum(np.where(amax > 0, np.frexp(amax)[1] - 1 + 127, 0) - down, 1)
    scale = np.exp2(byte - 127.0)
    codes = (blocks / scale).astype(np.float32).astype(dtype).astype(np.float64)
    return np.moveaxis((codes * scale).reshape(v.shape), -1, axis)


WIDE = False


def mx_kscale(k):
    if not WIDE:
        return np.ones(k)
    levels = np.array([10, -10, 5, -5, 0])
    if k % 512:
        return np.exp2(np.random.permutation(np.resize(levels, k // 32))).repeat(32)
    a = np.empty((k // 512, 16))
    for p in range(k // 512):
        a[p, :8] = np.random.permutation(np.resize(levels, 8))
        for g in range(8):
            far = levels[np.abs(levels - a[p, g]) >= 10]
            a[p, g + 8] = far[np.random.randint(len(far))]
    return np.exp2(a.ravel()).repeat(32)


def f64(x):
    return np.asarray(x).astype(np.float64)


def striped8(idx):
    return np.concatenate([v.reshape(-1, 16).T for v in idx]).astype(np.uint16)


def unstriped8(offs):
    return np.stack([offs[16 * g:16 * g + 16].T.reshape(-1) for g in range(8)]).astype(np.int64)


E2M1 = np.array([0.0, 0.5, 1.0, 1.5, 2.0, 3.0, 4.0, 6.0, -0.0, -0.5, -1.0, -1.5, -2.0, -3.0, -4.0, -6.0])


def pack_weight(w, fmt):
    k, n = w.shape
    w = f64(np.asarray(w, np.float32).astype(ml_dtypes.bfloat16)).reshape(k // 32, 32, n)
    amax = np.abs(w).max(1)
    if fmt == "e4m3":
        byte = np.frexp(amax)[1] - 1 + 127 - 7
    else:
        mant, ex = np.frexp(amax / 6.0)
        byte = np.where(mant > 0.5, ex, ex - 1) + 127
    byte = np.clip(np.where(amax > 0, byte, 1), 1, 254)
    scaled = (w * np.exp2(127.0 - byte)[:, None, :]).reshape(k, n).astype(np.float32)
    by_word = np.ascontiguousarray(scaled.reshape(k // 512, 128, 4, n).transpose(0, 1, 3, 2))
    if fmt == "e4m3":
        words = by_word.astype(ml_dtypes.float8_e4m3fn).view(np.uint8)
    else:
        c = by_word.astype(ml_dtypes.float4_e2m1fn).view(np.uint8) & 0xF
        words = (c[..., 0::2] | (c[..., 1::2] << 4)).reshape(k // 512, 128, 2 * n)
    return np.ascontiguousarray(words), np.ascontiguousarray(byte.astype(np.uint8).reshape(k // 512, 16, n))


def unpack_weight(words, scales, fmt):
    g, _, n = scales.shape
    words = np.ascontiguousarray(words).reshape(g, 128, n, -1)
    if fmt == "e4m3":
        vals = words.view(ml_dtypes.float8_e4m3fn).astype(np.float64)
    else:
        nib = np.empty((g, 128, n, 4), np.uint8)
        nib[..., 0::2] = words & 0xF
        nib[..., 1::2] = words >> 4
        vals = E2M1[nib]
    vals = vals * np.repeat(np.exp2(scales.astype(np.float64) - 127.0), 8, axis=1)[..., None]
    return vals.transpose(0, 1, 3, 2).reshape(g * 512, n)


G, K, M, T, S = 4, 512, 1024, 2048, 256


def setup_inputs():
    n = np.random.standard_normal
    s = mx_kscale(K)[:, None]
    p_w = pack_weight(n((K, M)) / np.sqrt(K) / s, "e2m1")
    return {
        "xT": (n((K, T)) * s).astype(np.float32),
        "w_words": p_w[0],
        "w_scales": p_w[1],
        "wgt": np.repeat(np.random.uniform(0.5, 2.0, (8, G * S)), 16, axis=0).astype(np.float32),
        "offs": striped8(np.stack([np.concatenate([np.random.permutation(T)[:S] for _ in range(G)]) for _ in range(8)])),
    }


def reference(xT, w_words, w_scales, wgt, offs):
    idx = unstriped8(offs)
    group = np.arange(K) % 512 // 64
    xg = f64(wgt)[np.arange(K) // 4 % 128] * f64(xT)[np.arange(K)[:, None], idx[group]]
    xT_ = mxq(xg, 0, "e4m3")
    xT_ = xT_.reshape(K, G, S).sum(1)
    w_ = unpack_weight(w_words, w_scales, "e2m1")
    y = xT_.T @ w_
    return y

from contextlib import ExitStack

import concourse.mybir as mybir

G, K, M, T, S = 4, 512, 1024, 2048, 256
FLOPS = 2 * G * K * M * S

F32 = mybir.dt.float32
BF16 = mybir.dt.bfloat16
I32 = mybir.dt.int32
U32 = mybir.dt.uint32
U16 = mybir.dt.uint16
U8 = mybir.dt.uint8
FP8X4 = mybir.dt.float8_e4m3fn_x4
FP4X4 = mybir.dt.float4_e2m1fn_x4
MULT = mybir.AluOpType.mult

P = 128
PACK = 4
J_TILE = 128
N_TILE = 512
LIST = 16
RING2 = 6
RING3 = 4


def tile_list_hbag_tm_none_kernel(tc, xT, w_words, w_scales, wgt, offs, out):
    nc = tc.nc
    with ExitStack() as ctx:
        keep = ctx.enter_context(tc.tile_pool(name="keep", bufs=1))
        psum = ctx.enter_context(tc.psum_pool(name="psum", bufs=1))

        offsets = keep.tile([P, G * S // LIST], U16, name="offsets")
        planes = [keep.tile([P, T], F32, name=f"plane{i}") for i in range(PACK)]
        wgt_first = keep.tile([P, S], F32, name="wgt_first")
        wgt_rest = keep.tile([P, (G - 1) * S], F32, name="wgt_rest")
        w_codes = keep.tile([P, 2 * M], U8, name="w_codes", align_bytes=64)
        w_scale = keep.tile([P, M], U8, name="w_scale", align_bytes=64)

        x_rows = xT.rearrange("(p i) t -> i p t", i=PACK)
        nc.vector.memset(w_scale[:].bitcast(I32), 0)
        nc.sync.dma_start(planes[0][:], x_rows[0])
        nc.sync.dma_start(offsets[:], offs)
        nc.sync.dma_start(wgt_first[:], wgt[:, 0:S])
        nc.sync.dma_start(wgt_rest[:], wgt[:, S : G * S])
        for i in range(1, PACK):
            nc.sync.dma_start(planes[i][:], x_rows[i])
        nc.sync.dma_start(w_codes[:].bitcast(I32), w_words[0].bitcast(I32))
        for q in range(4):
            nc.scalar.dma_start(
                w_scale[32 * q : 32 * q + 4, :].bitcast(I32), w_scales[0, 4 * q : 4 * q + 4, :].bitcast(I32)
            )

        def weights(c, j0, n):
            if c == 0:
                return wgt_first[:, j0 : j0 + n]
            return wgt_rest[:, (c - 1) * S + j0 : (c - 1) * S + j0 + n]

        def gather(dst, i, c, j0, n):
            first = (c * S + j0) // LIST
            picks = planes[i][:].indirect(offsets[:, first : first + n // LIST])
            nc.vector.tensor_tensor(dst, picks, weights(c, j0, n), MULT)

        low = [keep.tile([P, 2, S], F32, name=f"low{c}") for c in range(G)]
        high = [keep.tile([P, 3, J_TILE], F32, name=f"high{r}") for r in range(RING3)]
        woven = [keep.tile([P, S, PACK], BF16, name=f"woven{c}", align_bytes=64) for c in range(G)]

        for c in range(G):
            gather(low[c][:, 0, :], 0, c, 0, S)
        for c in range(G):
            gather(low[c][:, 1, :], 1, c, 0, S)
            nc.scalar.copy(woven[c][:, :, 0:2], low[c][:].rearrange("p i j -> p j i"))

        pieces = [(jt, c) for jt in range(S // J_TILE) for c in range(G)]

        def slot_of(k):
            return 0 if RING3 <= k < RING2 else 1

        def third(k):
            jt, c = pieces[k]
            gather(high[k % RING3][:, slot_of(k), :], 2, c, jt * J_TILE, J_TILE)

        for k in range(RING2):
            third(k)
        codes = {}
        scales = {}

        def finish(k):
            jt, c = pieces[k]
            j0 = jt * J_TILE
            slot2, slot3 = slot_of(k), 2
            gather(high[k % RING3][:, slot3, :], 3, c, j0, J_TILE)
            weave = nc.vector.tensor_copy if k == 0 else nc.scalar.copy
            weave(
                woven[c][:, j0 : j0 + J_TILE, 2:4],
                high[k % RING3][:, slot2 : slot3 + 1 : slot3 - slot2, :].rearrange("p i j -> p j i"),
            )

        def quantise(jt, c):
            j0 = jt * J_TILE
            codes[jt, c] = keep.tile([P, J_TILE], U32, name=f"codes{jt}{c}", align_bytes=64)
            scales[jt, c] = keep.tile([P, J_TILE], U8, name=f"scales{jt}{c}", align_bytes=64)
            nc.vector.quantize_mx(
                out=codes[jt, c][:].bitcast(FP8X4),
                scales=scales[jt, c][:],
                in_=woven[c][:, j0 : j0 + J_TILE, :].rearrange("p j i -> p (j i)"),
            )

        banks = {
            (jt, nh): psum.tile([P, N_TILE], F32, name=f"bank{jt}{nh}")
            for jt in range(S // J_TILE)
            for nh in range(M // N_TILE)
        }

        def multiply(jt, c, nh):
            n0 = nh * N_TILE
            nc.tensor.matmul_mx(
                out=banks[jt, nh][:],
                lhsT=codes[jt, c][:].bitcast(FP8X4),
                lhsT_scale=scales[jt, c][:],
                rhs=w_codes[:, 2 * n0 : 2 * (n0 + N_TILE)].bitcast(FP4X4),
                rhs_scale=w_scale[:, n0 : n0 + N_TILE],
                start=(c == 0),
                stop=(c == G - 1),
            )

        def store(jt, nh, n0, width, copy, queue):
            result = keep.tile([P, width], F32, name=f"result{jt}{nh}{n0}")
            copy(result[:], banks[jt, nh][:, n0 : n0 + width])
            first = nh * N_TILE + n0
            queue.dma_start(out[jt * J_TILE : (jt + 1) * J_TILE, first : first + width], result[:])

        for step in range(len(pieces) + RING3):
            if step > RING3:
                quantise(*pieces[step - RING3])
            if RING2 <= step < len(pieces):
                third(step)
            if step < len(pieces):
                finish(step)
            if step == 0:
                quantise(*pieces[0])
        for c in range(G):
            multiply(0, c, 0)
            multiply(0, c, 1)
        store(0, 0, 0, N_TILE, nc.scalar.copy, nc.sync)
        store(0, 1, 0, N_TILE, nc.vector.tensor_copy, nc.sync)
        for c, nh in [(0, 0), (0, 1), (1, 0), (1, 1), (2, 0), (3, 0), (2, 1), (3, 1)]:
            multiply(1, c, nh)
        store(1, 0, 0, N_TILE, nc.scalar.copy, nc.sync)
        store(1, 1, 0, N_TILE // 2, nc.vector.tensor_copy, nc.sync)
        store(1, 1, N_TILE // 2, N_TILE // 2, nc.vector.tensor_copy, nc.scalar)
